import numpy as np
import ml_dtypes


def mxq(x, axis, fmt="e4m3"):
    dtype, down = {"e4m3": (ml_dtypes.float8_e4m3fn, 7), "e5m2": (ml_dtypes.float8_e5m2, 14)}[fmt]
    v = np.moveaxis(np.asarray(x, np.float32).astype(ml_dtypes.bfloat16).astype(np.float64), axis, -1)
    blocks = v.reshape(v.shape[:-1] + (-1, 32))
    amax = np.abs(blocks).max(-1, keepdims=True)
    byte = np.maximum(np.where(amax > 0, np.frexp(amax)[1] - 1 + 127, 0) - down, 1)
    scale = np.exp2(byte - 127.0)
    codes = (blocks / scale).astype(np.float32).astype(dtype).astype(np.float64)
    return np.moveaxis((codes * scale).reshape(v.shape), -1, axis)


WIDE = False


def mx_kscale(k):
    if not WIDE:
        return np.ones(k)
    levels = np.array([10, -10, 5, -5, 0])
    if k % 512:
        return np.exp2(np.random.permutation(np.resize(levels, k // 32))).repeat(32)
    a = np.empty((k // 512, 16))
    for p in range(k // 512):
        a[p, :8] = np.random.permutation(np.resize(levels, 8))
        for g in range(8):
            far = levels[np.abs(levels - a[p, g]) >= 10]
            a[p, g + 8] = far[np.random.randint(len(far))]
    return np.exp2(a.ravel()).repeat(32)


def f64(x):
    return np.asarray(x).astype(np.float64)


def striped(idx):
    return np.tile(np.asarray(idx).reshape(-1, 16).T, (8, 1)).astype(np.uint16)


def unstriped(offs):
    return offs[:16].T.reshape(-1).astype(np.int64)


G, T, D, H = 1024, 2048, 512, 1024


def setup_inputs():
    n = np.random.standard_normal
    s = mx_kscale(D)[:, None]
    u = mx_kscale(H)[:, None]
    return {
        "xT": (n((D, T)) * s).astype(np.float32),
        "w1": (n((D, H)) / np.sqrt(D) / s * u[:, 0]).astype(np.float32),
        "w2": (n((H, D)) / np.sqrt(H) / u * s[:, 0]).astype(np.float32),
        "offs": striped(np.random.permutation(T)[:G]),
    }


def reference(xT, w1, w2, offs):
    x = f64(xT)
    idx = unstriped(offs)
    a = mxq(f64(w1), 0, "e4m3").T @ mxq(x[:, idx], 0, "e4m3")
    h = np.maximum(a, 0.0)
    y = x[:, idx] + (mxq(f64(w2), 0, "e4m3").T @ mxq(h, 0, "e4m3"))
    out = x.copy()
    out[:, idx] = y
    return out

@@ -1,0 +1,185 @@
+from contextlib import ExitStack
+
+import concourse.mybir as mybir
+
+D, T, G, H = 512, 2048, 1024, 1024
+FLOPS = 2 * 2 * D * H * G
+
+F32 = mybir.dt.float32
+BF16 = mybir.dt.bfloat16
+U32 = mybir.dt.uint32
+U16 = mybir.dt.uint16
+U8 = mybir.dt.uint8
+FP8X4 = mybir.dt.float8_e4m3fn_x4
+RELU = mybir.ActivationFunctionType.Relu
+MULT, ADD, MAX = mybir.AluOpType.mult, mybir.AluOpType.add, mybir.AluOpType.max
+
+P = 128
+PACK = 4
+K_PASS = P * PACK
+HALF = 512
+NB = 128
+HIDDEN_PASSES = H // K_PASS
+
+
+def tile_attend_mod_relu_kernel(tc, xT, w1, w2, offs, out):
+    nc = tc.nc
+    with ExitStack() as ctx:
+        keep = ctx.enter_context(tc.tile_pool(name="keep", bufs=1))
+        psum1 = ctx.enter_context(tc.psum_pool(name="psum1", bufs=4))
+        psum2 = ctx.enter_context(tc.psum_pool(name="psum2", bufs=4))
+
+        warm = keep.tile([P, 1], F32, name="warm")
+        nc.vector.memset(warm[:], 0.0)
+        nc.scalar.activation(warm[:], warm[:], RELU)
+
+        offsets = keep.tile([P, G // 16], U16, name="offsets")
+        nc.sync.dma_start(offsets[:], offs)
+        planes = []
+        x_rows = xT.rearrange("(p t) c -> t p c", t=PACK)
+        out_rows = out.rearrange("(p t) c -> t p c", t=PACK)
+        for t in range(PACK):
+            plane = keep.tile([P, T], F32, name=f"plane{t}")
+            nc.sync.dma_start(plane[:], x_rows[t])
+            planes.append(plane)
+
+        w1_raw, w2_raw = [], []
+        w1_rows = w1.rearrange("(p j) c -> p j c", j=PACK)
+        for g in range(HIDDEN_PASSES):
+            raw = keep.tile([P, PACK, K_PASS], F32, name=f"w1_raw{g}")
+            nc.sync.dma_start(raw[:], w1_rows[:, :, g * K_PASS : (g + 1) * K_PASS])
+            w1_raw.append(raw)
+        for g in range(HIDDEN_PASSES):
+            raw = keep.tile([P, PACK, D], F32, name=f"w2_raw{g}")
+            nc.sync.dma_start(raw[:], w2[g * K_PASS : (g + 1) * K_PASS, :].rearrange("(p j) c -> p j c", j=PACK))
+            w2_raw.append(raw)
+
+        def group_views(raw, grouped, m0, m1):
+            dst = grouped[:].rearrange("p (t m j) -> p m t j", t=PACK, j=PACK)[:, m0:m1]
+            src = raw[:].rearrange("p j (m t) -> p m t j", t=PACK)[:, m0:m1]
+            return dst, src
+
+        def on_vector(dst, src):
+            nc.vector.tensor_copy(dst, src)
+
+        def on_scalar(dst, src):
+            nc.scalar.copy(dst, src)
+
+        def on_gpsimd(dst, src):
+            nc.gpsimd.tensor_scalar(dst, src, 1.0, 0.0, MULT, ADD)
+
+        def group_weight(raw, label, shares):
+            grouped = keep.tile([P, K_PASS * PACK], BF16, align_bytes=64, name=f"{label}_grouped")
+            for engine, m0, m1 in shares:
+                engine(*group_views(raw, grouped, m0, m1))
+            return grouped
+
+        def quantize(grouped, label):
+            codes = keep.tile([P, K_PASS], U32, align_bytes=64, name=f"{label}_codes")
+            scales = keep.tile([P, K_PASS], U8, align_bytes=64, name=f"{label}_scales")
+            nc.vector.quantize_mx(out=codes[:].bitcast(FP8X4), scales=scales[:], in_=grouped[:])
+            return codes, scales
+
+        picked = [keep.tile([P, PACK, HALF], F32, name=f"picked{h}") for h in range(2)]
+        for t in range(PACK):
+            for h in range(2):
+                nc.vector.tensor_copy(
+                    picked[h][:, t, :], planes[t][:].indirect(offsets[:, h * HALF // 16 : (h + 1) * HALF // 16])
+                )
+
+        def group_x(h, engine):
+            grouped = keep.tile([P, HALF * PACK], BF16, align_bytes=64, name=f"x{h}_grouped")
+            engine(
+                grouped[:].rearrange("p (c i t) -> p c t i", i=4, t=PACK),
+                picked[h][:].rearrange("p t (c i) -> p c t i", i=4),
+            )
+            return grouped
+
+        def first_layer(h, g, x_mx, w_mx, engines):
+            grouped = keep.tile([P, HALF, PACK], BF16, align_bytes=64, name=f"h{h}{g}_grouped")
+            for b in range(HALF // NB):
+                cols = slice(b * NB, (b + 1) * NB)
+                acc = psum1.tile([P, PACK, NB], F32, name="acc1")
+                for t in range(PACK):
+                    chans = slice(t * P, (t + 1) * P)
+                    nc.tensor.matmul_mx(
+                        out=acc[:, t, :],
+                        lhsT=w_mx[0][:, chans].bitcast(FP8X4),
+                        lhsT_scale=w_mx[1][:, chans],
+                        rhs=x_mx[0][:, cols].bitcast(FP8X4),
+                        rhs_scale=x_mx[1][:, cols],
+                        start=True,
+                        stop=True,
+                    )
+                src = acc[:].rearrange("p t n -> p n t")
+                if engines[b] == "v":
+                    nc.vector.tensor_scalar_max(grouped[:, cols, :], src, 0.0)
+                else:
+                    nc.scalar.activation(grouped[:, cols, :], src, RELU)
+            return grouped
+
+        def quantize_h(grouped, label):
+            codes = keep.tile([P, HALF], U32, align_bytes=64, name=f"{label}_codes")
+            scales = keep.tile([P, HALF], U8, align_bytes=64, name=f"{label}_scales")
+            nc.vector.quantize_mx(
+                out=codes[:].bitcast(FP8X4), scales=scales[:], in_=grouped[:].rearrange("p n t -> p (n t)")
+            )
+            return codes, scales
+
+        def second_layer(t, h_mx):
+            acc = psum2.tile([P, HALF], F32, name="acc2")
+            chans = slice(t * P, (t + 1) * P)
+            for g in range(HIDDEN_PASSES):
+                nc.tensor.matmul_mx(
+                    out=acc[:],
+                    lhsT=w2_mx[g][0][:, chans].bitcast(FP8X4),
+                    lhsT_scale=w2_mx[g][1][:, chans],
+                    rhs=h_mx[g][0][:].bitcast(FP8X4),
+                    rhs_scale=h_mx[g][1][:],
+                    start=(g == 0),
+                    stop=(g == HIDDEN_PASSES - 1),
+                )
+            return acc
+
+        def add(h, t, acc):
+            y = keep.tile([P, HALF], F32, name=f"y{h}{t}")
+            nc.vector.tensor_tensor(y[:], acc[:], picked[h][:, t, :], ADD)
+            return y
+
+        def scatter(h, t, y):
+            nc.vector.tensor_copy(planes[t][:].indirect(offsets[:, h * HALF // 16 : (h + 1) * HALF // 16]), y[:])
+
+        xa = group_x(0, on_scalar)
+        w1a = group_weight(w1_raw[0], "w1a", [(on_vector, 0, P)])
+        xa_mx = quantize(xa, "xa")
+        w1_mx = [quantize(w1a, "w1a")]
+        ha0 = first_layer(0, 0, xa_mx, w1_mx[0], "svsv")
+        w1b = group_weight(w1_raw[1], "w1b", [(on_gpsimd, 0, P // 2), (on_scalar, P // 2, P)])
+        w1_mx.append(quantize(w1b, "w1b"))
+        ha1 = first_layer(0, 1, xa_mx, w1_mx[1], "svsv")
+        w2a = group_weight(w2_raw[0], "w2a", [(on_gpsimd, 0, P)])
+        ha_mx = [quantize_h(ha0, "ha0"), quantize_h(ha1, "ha1")]
+        xb = group_x(1, on_scalar)
+        w2b = group_weight(w2_raw[1], "w2b", [(on_vector, 0, P // 2), (on_scalar, P // 2, P)])
+        w2_mx = [quantize(w2a, "w2a"), quantize(w2b, "w2b")]
+        acc_a = [second_layer(t, ha_mx) for t in range(PACK)]
+
+        y0 = add(0, 0, acc_a[0])
+        y1 = add(0, 1, acc_a[1])
+        scatter(0, 0, y0)
+        xb_mx = quantize(xb, "xb")
+        hb0 = first_layer(1, 0, xb_mx, w1_mx[0], "ssss")
+        hb1 = first_layer(1, 1, xb_mx, w1_mx[1], "ssss")
+        y2 = add(0, 2, acc_a[2])
+        scatter(0, 1, y1)
+        y3 = add(0, 3, acc_a[3])
+        scatter(0, 2, y2)
+        hb_mx = [quantize_h(hb0, "hb0"), quantize_h(hb1, "hb1")]
+        scatter(0, 3, y3)
+        acc_b = [second_layer(t, hb_mx) for t in range(PACK)]
+        z = add(1, 0, acc_b[0])
+        for t in range(PACK):
+            z_next = add(1, t + 1, acc_b[t + 1]) if t + 1 < PACK else None
+            scatter(1, t, z)
+            nc.sync.dma_start(out_rows[t], planes[t][:])
+            z = z_next

@@ -35,24 +35,30 @@ def tile_attend_mod_relu_kernel(tc, xT, w1, w2, offs, out):
 
         offsets = keep.tile([P, G // 16], U16, name="offsets")
         nc.sync.dma_start(offsets[:], offs)
-        planes = []
         x_rows = xT.rearrange("(p t) c -> t p c", t=PACK)
         out_rows = out.rearrange("(p t) c -> t p c", t=PACK)
-        for t in range(PACK):
-            plane = keep.tile([P, T], F32, name=f"plane{t}")
-            nc.sync.dma_start(plane[:], x_rows[t])
-            planes.append(plane)
-
-        w1_raw, w2_raw = [], []
         w1_rows = w1.rearrange("(p j) c -> p j c", j=PACK)
-        for g in range(HIDDEN_PASSES):
-            raw = keep.tile([P, PACK, K_PASS], F32, name=f"w1_raw{g}")
-            nc.sync.dma_start(raw[:], w1_rows[:, :, g * K_PASS : (g + 1) * K_PASS])
-            w1_raw.append(raw)
-        for g in range(HIDDEN_PASSES):
-            raw = keep.tile([P, PACK, D], F32, name=f"w2_raw{g}")
-            nc.sync.dma_start(raw[:], w2[g * K_PASS : (g + 1) * K_PASS, :].rearrange("(p j) c -> p j c", j=PACK))
-            w2_raw.append(raw)
+        planes = [keep.tile([P, T], F32, name=f"plane{t}") for t in range(PACK)]
+        w1_raw = [keep.tile([P, PACK, K_PASS], F32, name=f"w1_raw{g}") for g in range(HIDDEN_PASSES)]
+        w2_raw = [keep.tile([P, PACK, D], F32, name=f"w2_raw{g}") for g in range(HIDDEN_PASSES)]
+
+        def load_x(t):
+            nc.sync.dma_start(planes[t][:], x_rows[t])
+
+        def load_w1(g):
+            nc.sync.dma_start(w1_raw[g][:], w1_rows[:, :, g * K_PASS : (g + 1) * K_PASS])
+
+        def load_w2(g, c0, c1):
+            rows = w2[g * K_PASS : (g + 1) * K_PASS, :].rearrange("(p j) c -> p j c", j=PACK)
+            nc.sync.dma_start(w2_raw[g][:, :, c0:c1], rows[:, :, c0:c1])
+
+        for t in range(PACK):
+            load_x(t)
+        load_w1(0)
+        load_w1(1)
+        load_w2(0, 0, D)
+        load_w2(1, 0, D // 2)
+        load_w2(1, D // 2, D)
 
         def group_views(raw, grouped, m0, m1):
             dst = grouped[:].rearrange("p (t m j) -> p m t j", t=PACK, j=PACK)[:, m0:m1]
@@ -68,8 +74,8 @@ def tile_attend_mod_relu_kernel(tc, xT, w1, w2, offs, out):
         def on_gpsimd(dst, src):
             nc.gpsimd.tensor_scalar(dst, src, 1.0, 0.0, MULT, ADD)
 
-        def group_weight(raw, label, shares):
-            grouped = keep.tile([P, K_PASS * PACK], BF16, align_bytes=64, name=f"{label}_grouped")
+        def group_weight(raw, label, tag, shares):
+            grouped = keep.tile([P, K_PASS * PACK], BF16, align_bytes=64, tag=tag, name=f"{label}_grouped")
             for engine, m0, m1 in shares:
                 engine(*group_views(raw, grouped, m0, m1))
             return grouped
@@ -80,23 +86,26 @@ def tile_attend_mod_relu_kernel(tc, xT, w1, w2, offs, out):
             nc.vector.quantize_mx(out=codes[:].bitcast(FP8X4), scales=scales[:], in_=grouped[:])
             return codes, scales
 
-        picked = [keep.tile([P, PACK, HALF], F32, name=f"picked{h}") for h in range(2)]
-        for t in range(PACK):
-            for h in range(2):
-                nc.vector.tensor_copy(
-                    picked[h][:, t, :], planes[t][:].indirect(offsets[:, h * HALF // 16 : (h + 1) * HALF // 16])
-                )
-
-        def group_x(h, engine):
-            grouped = keep.tile([P, HALF * PACK], BF16, align_bytes=64, name=f"x{h}_grouped")
-            engine(
-                grouped[:].rearrange("p (c i t) -> p c t i", i=4, t=PACK),
-                picked[h][:].rearrange("p t (c i) -> p c t i", i=4),
+        def quantize_3d(grouped, label, tag):
+            codes = keep.tile([P, HALF], U32, align_bytes=64, tag=tag, name=f"{label}_codes")
+            scales = keep.tile([P, HALF], U8, align_bytes=64, name=f"{label}_scales")
+            nc.vector.quantize_mx(
+                out=codes[:].bitcast(FP8X4), scales=scales[:], in_=grouped[:].rearrange("p n t -> p (n t)")
             )
-            return grouped
+            return codes, scales
 
-        def first_layer(h, g, x_mx, w_mx, engines):
-            grouped = keep.tile([P, HALF, PACK], BF16, align_bytes=64, name=f"h{h}{g}_grouped")
+        picked = keep.tile([P, PACK, G], F32, name="picked")
+
+        def gather(t, n0, n1):
+            nc.vector.tensor_copy(picked[:, t, n0:n1], planes[t][:].indirect(offsets[:, n0 // 16 : n1 // 16]))
+
+        def group_x(grouped, h, engine, t0, t1):
+            engine(
+                grouped[:, :, t0:t1],
+                picked[:, t0:t1, h * HALF : (h + 1) * HALF].rearrange("p t n -> p n t"),
+            )
+
+        def first_layer(grouped, x_mx, w_mx, engines):
             for b in range(HALF // NB):
                 cols = slice(b * NB, (b + 1) * NB)
                 acc = psum1.tile([P, PACK, NB], F32, name="acc1")
@@ -116,15 +125,6 @@ def tile_attend_mod_relu_kernel(tc, xT, w1, w2, offs, out):
                     nc.vector.tensor_scalar_max(grouped[:, cols, :], src, 0.0)
                 else:
                     nc.scalar.activation(grouped[:, cols, :], src, RELU)
-            return grouped
-
-        def quantize_h(grouped, label):
-            codes = keep.tile([P, HALF], U32, align_bytes=64, name=f"{label}_codes")
-            scales = keep.tile([P, HALF], U8, align_bytes=64, name=f"{label}_scales")
-            nc.vector.quantize_mx(
-                out=codes[:].bitcast(FP8X4), scales=scales[:], in_=grouped[:].rearrange("p n t -> p (n t)")
-            )
-            return codes, scales
 
         def second_layer(t, h_mx):
             acc = psum2.tile([P, HALF], F32, name="acc2")
@@ -141,45 +141,68 @@ def tile_attend_mod_relu_kernel(tc, xT, w1, w2, offs, out):
                 )
             return acc
 
-        def add(h, t, acc):
-            y = keep.tile([P, HALF], F32, name=f"y{h}{t}")
-            nc.vector.tensor_tensor(y[:], acc[:], picked[h][:, t, :], ADD)
+        def add(h, t, acc, tag):
+            y = keep.tile([P, HALF], F32, align_bytes=64, tag=tag, name=f"y{h}{t}")
+            nc.vector.tensor_tensor(y[:], acc[:], picked[:, t, h * HALF : (h + 1) * HALF], ADD)
+            return y
+
+        def add_apart(h, t, acc, tag):
+            product = keep.tile([P, HALF], F32, name=f"product{h}{t}")
+            nc.scalar.copy(product[:], acc[:])
+            y = keep.tile([P, HALF], F32, align_bytes=64, tag=tag, name=f"y{h}{t}")
+            nc.gpsimd.tensor_tensor(y[:], product[:], picked[:, t, h * HALF : (h + 1) * HALF], ADD)
             return y
 
         def scatter(h, t, y):
             nc.vector.tensor_copy(planes[t][:].indirect(offsets[:, h * HALF // 16 : (h + 1) * HALF // 16]), y[:])
 
-        xa = group_x(0, on_scalar)
-        w1a = group_weight(w1_raw[0], "w1a", [(on_vector, 0, P)])
-        xa_mx = quantize(xa, "xa")
+        for t in range(PACK - 1):
+            gather(t, 0, G)
+        gather(PACK - 1, 0, HALF)
+        gather(PACK - 1, HALF, G)
+        xa = keep.tile([P, HALF, PACK], BF16, align_bytes=64, tag="slot_a", name="xa_grouped")
+        xb = keep.tile([P, HALF, PACK], BF16, align_bytes=64, name="xb_grouped")
+        group_x(xa, 0, on_scalar, 0, 2)
+        group_x(xb, 1, on_scalar, 0, 2)
+        group_x(xa, 0, on_scalar, 2, 4)
+        w1a = group_weight(w1_raw[0], "w1a", "slot_b", [(on_gpsimd, 0, 96), (on_vector, 96, P)])
+        xa_mx = quantize_3d(xa, "xa", "x_codes")
         w1_mx = [quantize(w1a, "w1a")]
-        ha0 = first_layer(0, 0, xa_mx, w1_mx[0], "svsv")
-        w1b = group_weight(w1_raw[1], "w1b", [(on_gpsimd, 0, P // 2), (on_scalar, P // 2, P)])
+        group_x(xb, 1, on_scalar, 2, 4)
+        ha0 = keep.tile([P, HALF, PACK], BF16, align_bytes=64, name="ha0_grouped")
+        first_layer(ha0, xa_mx, w1_mx[0], "ssss")
+        w1b = group_weight(w1_raw[1], "w1b", "slot_a", [(on_gpsimd, 0, 96), (on_vector, 96, P)])
         w1_mx.append(quantize(w1b, "w1b"))
-        ha1 = first_layer(0, 1, xa_mx, w1_mx[1], "svsv")
-        w2a = group_weight(w2_raw[0], "w2a", [(on_gpsimd, 0, P)])
-        ha_mx = [quantize_h(ha0, "ha0"), quantize_h(ha1, "ha1")]
-        xb = group_x(1, on_scalar)
-        w2b = group_weight(w2_raw[1], "w2b", [(on_vector, 0, P // 2), (on_scalar, P // 2, P)])
-        w2_mx = [quantize(w2a, "w2a"), quantize(w2b, "w2b")]
+        ha1 = keep.tile([P, HALF, PACK], BF16, align_bytes=64, name="ha1_grouped")
+        first_layer(ha1, xa_mx, w1_mx[1], "ssss")
+        ha_mx = [quantize_3d(ha0, "ha0", "ha0_codes")]
+        xb_mx = quantize_3d(xb, "xb", "x_codes")
+        w2a = group_weight(w2_raw[0], "w2a", "slot_b", [(on_gpsimd, 0, 96), (on_vector, 96, P)])
+        w2_mx = [quantize(w2a, "w2a")]
+        w2b = group_weight(w2_raw[1], "w2b", "slot_a", [(on_gpsimd, 0, 64), (on_vector, 64, P)])
+        ha_mx.append(quantize_3d(ha1, "ha1", "ha1_codes"))
+        w2_mx.append(quantize(w2b, "w2b"))
         acc_a = [second_layer(t, ha_mx) for t in range(PACK)]
-
-        y0 = add(0, 0, acc_a[0])
-        y1 = add(0, 1, acc_a[1])
+        y0 = add(0, 0, acc_a[0], "y00")
+        y1 = add_apart(0, 1, acc_a[1], "y01")
         scatter(0, 0, y0)
-        xb_mx = quantize(xb, "xb")
-        hb0 = first_layer(1, 0, xb_mx, w1_mx[0], "ssss")
-        hb1 = first_layer(1, 1, xb_mx, w1_mx[1], "ssss")
-        y2 = add(0, 2, acc_a[2])
+        hb = keep.tile([P, HIDDEN_PASSES, HALF, PACK], BF16, align_bytes=64, tag="slot_e", name="hb_grouped")
+        first_layer(hb[:, 0], xb_mx, w1_mx[0], "ssss")
+        y2 = add_apart(0, 2, acc_a[2], "y02")
+        first_layer(hb[:, 1], xb_mx, w1_mx[1], "ssss")
         scatter(0, 1, y1)
-        y3 = add(0, 3, acc_a[3])
+        hb_codes = keep.tile([P, HIDDEN_PASSES, HALF], U32, align_bytes=64, name="hb_codes")
+        hb_scales = keep.tile([P, HIDDEN_PASSES, HALF], U8, align_bytes=64, name="hb_scales")
+        nc.vector.quantize_mx(
+            out=hb_codes[:].rearrange("p g n -> p (g n)").bitcast(FP8X4),
+            scales=hb_scales[:].rearrange("p g n -> p (g n)"),
+            in_=hb[:].rearrange("p g n t -> p (g n t)"),
+        )
+        hb_mx = [(hb_codes[:, g], hb_scales[:, g]) for g in range(HIDDEN_PASSES)]
         scatter(0, 2, y2)
-        hb_mx = [quantize_h(hb0, "hb0"), quantize_h(hb1, "hb1")]
+        y3 = add(0, 3, acc_a[3], "slot_e")
         scatter(0, 3, y3)
-        acc_b = [second_layer(t, hb_mx) for t in range(PACK)]
-        z = add(1, 0, acc_b[0])
         for t in range(PACK):
-            z_next = add(1, t + 1, acc_b[t + 1]) if t + 1 < PACK else None
-            scatter(1, t, z)
+            y_b = add_apart(1, t, second_layer(t, hb_mx), f"y1{t}")
+            scatter(1, t, y_b)
             nc.sync.dma_start(out_rows[t], planes[t][:])
-            z = z_next

from contextlib import ExitStack

import concourse.mybir as mybir

D, T, G, H = 512, 2048, 1024, 1024
FLOPS = 2 * 2 * D * H * G

F32 = mybir.dt.float32
BF16 = mybir.dt.bfloat16
U32 = mybir.dt.uint32
U16 = mybir.dt.uint16
U8 = mybir.dt.uint8
FP8X4 = mybir.dt.float8_e4m3fn_x4
RELU = mybir.ActivationFunctionType.Relu
MULT, ADD, MAX = mybir.AluOpType.mult, mybir.AluOpType.add, mybir.AluOpType.max

P = 128
PACK = 4
K_PASS = P * PACK
HALF = 512
NB = 128
HIDDEN_PASSES = H // K_PASS


def tile_attend_mod_relu_kernel(tc, xT, w1, w2, offs, out):
    nc = tc.nc
    with ExitStack() as ctx:
        keep = ctx.enter_context(tc.tile_pool(name="keep", bufs=1))
        psum1 = ctx.enter_context(tc.psum_pool(name="psum1", bufs=4))
        psum2 = ctx.enter_context(tc.psum_pool(name="psum2", bufs=4))

        warm = keep.tile([P, 1], F32, name="warm")
        nc.vector.memset(warm[:], 0.0)
        nc.scalar.activation(warm[:], warm[:], RELU)

        offsets = keep.tile([P, G // 16], U16, name="offsets")
        nc.sync.dma_start(offsets[:], offs)
        x_rows = xT.rearrange("(p t) c -> t p c", t=PACK)
        out_rows = out.rearrange("(p t) c -> t p c", t=PACK)
        w1_rows = w1.rearrange("(p j) c -> p j c", j=PACK)
        planes = [keep.tile([P, T], F32, name=f"plane{t}") for t in range(PACK)]
        w1_raw = [keep.tile([P, PACK, K_PASS], F32, name=f"w1_raw{g}") for g in range(HIDDEN_PASSES)]
        w2_raw = [keep.tile([P, PACK, D], F32, name=f"w2_raw{g}") for g in range(HIDDEN_PASSES)]

        def load_x(t):
            nc.sync.dma_start(planes[t][:], x_rows[t])

        def load_w1(g):
            nc.sync.dma_start(w1_raw[g][:], w1_rows[:, :, g * K_PASS : (g + 1) * K_PASS])

        def load_w2(g, c0, c1):
            rows = w2[g * K_PASS : (g + 1) * K_PASS, :].rearrange("(p j) c -> p j c", j=PACK)
            nc.sync.dma_start(w2_raw[g][:, :, c0:c1], rows[:, :, c0:c1])

        for t in range(PACK):
            load_x(t)
        load_w1(0)
        load_w1(1)
        load_w2(0, 0, D)
        load_w2(1, 0, D // 2)
        load_w2(1, D // 2, D)

        def group_views(raw, grouped, m0, m1):
            dst = grouped[:].rearrange("p (t m j) -> p m t j", t=PACK, j=PACK)[:, m0:m1]
            src = raw[:].rearrange("p j (m t) -> p m t j", t=PACK)[:, m0:m1]
            return dst, src

        def on_vector(dst, src):
            nc.vector.tensor_copy(dst, src)

        def on_scalar(dst, src):
            nc.scalar.copy(dst, src)

        def on_gpsimd(dst, src):
            nc.gpsimd.tensor_scalar(dst, src, 1.0, 0.0, MULT, ADD)

        def group_weight(raw, label, tag, shares):
            grouped = keep.tile([P, K_PASS * PACK], BF16, align_bytes=64, tag=tag, name=f"{label}_grouped")
            for engine, m0, m1 in shares:
                engine(*group_views(raw, grouped, m0, m1))
            return grouped

        def quantize(grouped, label):
            codes = keep.tile([P, K_PASS], U32, align_bytes=64, name=f"{label}_codes")
            scales = keep.tile([P, K_PASS], U8, align_bytes=64, name=f"{label}_scales")
            nc.vector.quantize_mx(out=codes[:].bitcast(FP8X4), scales=scales[:], in_=grouped[:])
            return codes, scales

        def quantize_3d(grouped, label, tag):
            codes = keep.tile([P, HALF], U32, align_bytes=64, tag=tag, name=f"{label}_codes")
            scales = keep.tile([P, HALF], U8, align_bytes=64, name=f"{label}_scales")
            nc.vector.quantize_mx(
                out=codes[:].bitcast(FP8X4), scales=scales[:], in_=grouped[:].rearrange("p n t -> p (n t)")
            )
            return codes, scales

        picked = keep.tile([P, PACK, G], F32, name="picked")

        def gather(t, n0, n1):
            nc.vector.tensor_copy(picked[:, t, n0:n1], planes[t][:].indirect(offsets[:, n0 // 16 : n1 // 16]))

        def group_x(grouped, h, engine, t0, t1):
            engine(
                grouped[:, :, t0:t1],
                picked[:, t0:t1, h * HALF : (h + 1) * HALF].rearrange("p t n -> p n t"),
            )

        def first_layer(grouped, x_mx, w_mx, engines):
            for b in range(HALF // NB):
                cols = slice(b * NB, (b + 1) * NB)
                acc = psum1.tile([P, PACK, NB], F32, name="acc1")
                for t in range(PACK):
                    chans = slice(t * P, (t + 1) * P)
                    nc.tensor.matmul_mx(
                        out=acc[:, t, :],
                        lhsT=w_mx[0][:, chans].bitcast(FP8X4),
                        lhsT_scale=w_mx[1][:, chans],
                        rhs=x_mx[0][:, cols].bitcast(FP8X4),
                        rhs_scale=x_mx[1][:, cols],
                        start=True,
                        stop=True,
                    )
                src = acc[:].rearrange("p t n -> p n t")
                if engines[b] == "v":
                    nc.vector.tensor_scalar_max(grouped[:, cols, :], src, 0.0)
                else:
                    nc.scalar.activation(grouped[:, cols, :], src, RELU)

        def second_layer(t, h_mx):
            acc = psum2.tile([P, HALF], F32, name="acc2")
            chans = slice(t * P, (t + 1) * P)
            for g in range(HIDDEN_PASSES):
                nc.tensor.matmul_mx(
                    out=acc[:],
                    lhsT=w2_mx[g][0][:, chans].bitcast(FP8X4),
                    lhsT_scale=w2_mx[g][1][:, chans],
                    rhs=h_mx[g][0][:].bitcast(FP8X4),
                    rhs_scale=h_mx[g][1][:],
                    start=(g == 0),
                    stop=(g == HIDDEN_PASSES - 1),
                )
            return acc

        def add(h, t, acc, tag):
            y = keep.tile([P, HALF], F32, align_bytes=64, tag=tag, name=f"y{h}{t}")
            nc.vector.tensor_tensor(y[:], acc[:], picked[:, t, h * HALF : (h + 1) * HALF], ADD)
            return y

        def add_apart(h, t, acc, tag):
            product = keep.tile([P, HALF], F32, name=f"product{h}{t}")
            nc.scalar.copy(product[:], acc[:])
            y = keep.tile([P, HALF], F32, align_bytes=64, tag=tag, name=f"y{h}{t}")
            nc.gpsimd.tensor_tensor(y[:], product[:], picked[:, t, h * HALF : (h + 1) * HALF], ADD)
            return y

        def scatter(h, t, y):
            nc.vector.tensor_copy(planes[t][:].indirect(offsets[:, h * HALF // 16 : (h + 1) * HALF // 16]), y[:])

        for t in range(PACK - 1):
            gather(t, 0, G)
        gather(PACK - 1, 0, HALF)
        gather(PACK - 1, HALF, G)
        xa = keep.tile([P, HALF, PACK], BF16, align_bytes=64, tag="slot_a", name="xa_grouped")
        xb = keep.tile([P, HALF, PACK], BF16, align_bytes=64, name="xb_grouped")
        group_x(xa, 0, on_scalar, 0, 2)
        group_x(xb, 1, on_scalar, 0, 2)
        group_x(xa, 0, on_scalar, 2, 4)
        w1a = group_weight(w1_raw[0], "w1a", "slot_b", [(on_gpsimd, 0, 96), (on_vector, 96, P)])
        xa_mx = quantize_3d(xa, "xa", "x_codes")
        w1_mx = [quantize(w1a, "w1a")]
        group_x(xb, 1, on_scalar, 2, 4)
        ha0 = keep.tile([P, HALF, PACK], BF16, align_bytes=64, name="ha0_grouped")
        first_layer(ha0, xa_mx, w1_mx[0], "ssss")
        w1b = group_weight(w1_raw[1], "w1b", "slot_a", [(on_gpsimd, 0, 96), (on_vector, 96, P)])
        w1_mx.append(quantize(w1b, "w1b"))
        ha1 = keep.tile([P, HALF, PACK], BF16, align_bytes=64, name="ha1_grouped")
        first_layer(ha1, xa_mx, w1_mx[1], "ssss")
        ha_mx = [quantize_3d(ha0, "ha0", "ha0_codes")]
        xb_mx = quantize_3d(xb, "xb", "x_codes")
        w2a = group_weight(w2_raw[0], "w2a", "slot_b", [(on_gpsimd, 0, 96), (on_vector, 96, P)])
        w2_mx = [quantize(w2a, "w2a")]
        w2b = group_weight(w2_raw[1], "w2b", "slot_a", [(on_gpsimd, 0, 64), (on_vector, 64, P)])
        ha_mx.append(quantize_3d(ha1, "ha1", "ha1_codes"))
        w2_mx.append(quantize(w2b, "w2b"))
        acc_a = [second_layer(t, ha_mx) for t in range(PACK)]
        y0 = add(0, 0, acc_a[0], "y00")
        y1 = add_apart(0, 1, acc_a[1], "y01")
        scatter(0, 0, y0)
        hb = keep.tile([P, HIDDEN_PASSES, HALF, PACK], BF16, align_bytes=64, tag="slot_e", name="hb_grouped")
        first_layer(hb[:, 0], xb_mx, w1_mx[0], "ssss")
        y2 = add_apart(0, 2, acc_a[2], "y02")
        first_layer(hb[:, 1], xb_mx, w1_mx[1], "ssss")
        scatter(0, 1, y1)
        hb_codes = keep.tile([P, HIDDEN_PASSES, HALF], U32, align_bytes=64, name="hb_codes")
        hb_scales = keep.tile([P, HIDDEN_PASSES, HALF], U8, align_bytes=64, name="hb_scales")
        nc.vector.quantize_mx(
            out=hb_codes[:].rearrange("p g n -> p (g n)").bitcast(FP8X4),
            scales=hb_scales[:].rearrange("p g n -> p (g n)"),
            in_=hb[:].rearrange("p g n t -> p (g n t)"),
        )
        hb_mx = [(hb_codes[:, g], hb_scales[:, g]) for g in range(HIDDEN_PASSES)]
        scatter(0, 2, y2)
        y3 = add(0, 3, acc_a[3], "slot_e")
        scatter(0, 3, y3)
        for t in range(PACK):
            y_b = add_apart(1, t, second_layer(t, hb_mx), f"y1{t}")
            scatter(1, t, y_b)
            nc.sync.dma_start(out_rows[t], planes[t][:])
